import numpy as np, ml_dtypes
CORES = [2,6,10,14,18,22,26,30]
N = 8
import mx_ref
BF = ml_dtypes.bfloat16
def entries(a):
    return np.ascontiguousarray(a.T).reshape(-1)
def table(e):
    return np.ascontiguousarray(np.reshape(e, (-1, 16)).T).astype(np.int32)
def gcols(t, e):
    v = np.concatenate([t.reshape(8, 16, -1, 4), np.zeros((8, 16, 1, 4), BF)], axis=2)
    return np.ascontiguousarray(np.stack([v[g][:, e[g]] for g in range(8)])).reshape(128, -1)
def cut(t, i, w=512):
    return t[:, w * i:w * i + w]
def f(rng, *shape):
    return mx_ref.flush((rng.standard_normal(shape, dtype=np.float32) * np.exp2(rng.integers(-2, 3, shape[:-1] + (1,)))).astype(BF))
def wide(rng, *shape, cols=0):
    v = rng.standard_normal(shape, dtype=np.float32) * np.exp2(rng.integers(-12, 13, shape)).astype(np.float32)
    if cols: v *= np.repeat(np.exp2(rng.integers(-cols, cols + 1, shape[:-2] + (1, shape[-1] // 4))) * (rng.random(shape[:-2] + (1, shape[-1] // 4)) > 0.0625), 4, axis=-1).astype(np.float32)
    return mx_ref.flush(v.astype(BF))
K, T, O = 256, 256, 4
SH = (7, 6, 5, 4, 3, 2, 1, 0)
A = (1531, 797, 1877, 1129, 619, 1993, 1367, 911)
B = (1013, 1741, 587, 1459, 1907, 733, 1229, 1667)
def levels(q):
    return list(range(8 // N * q, 8 // N * (q + 1)))
def owned(t):
    t = t.reshape(N, 8, 16, -1).copy()
    for q in range(N):
        for g in range(8):
            if g not in levels(q): t[q, g] = 0
    return t.reshape(N, 128, -1)
def pack(p):
    return np.stack([table(p[r]) for r in range(N)])
def places(rng):
    return {"px": pack(rng.integers(0, 1024, (N, T))), "py": pack(rng.integers(0, 1024, (N, T)))}
def setup_inputs(rng):
    return {"tb": owned(f(rng, N, 128, 4 * K)), **places(rng), "w": f(rng, N, 128, 512 * O)}
def setup_inputs_same(rng):
    d = setup_inputs(rng)
    d["px"] = pack(np.repeat(rng.integers(0, 1024, (N, 1)), T, axis=1)); d["py"] = pack(np.repeat(rng.integers(0, 1024, (N, 1)), T, axis=1))
    return d
def setup_inputs_corner(rng):
    d = setup_inputs(rng); c = rng.integers(0, 4, (N, T))
    for r in range(N): c[r, rng.permutation(T)[:4]] = np.arange(4)
    d["px"] = pack((c & 1) * 1023); d["py"] = pack((c >> 1) * 1023)
    return d
def setup_inputs_alike(rng):
    d = setup_inputs(rng)
    d["px"] = pack(np.repeat(rng.integers(0, 1024, (1, T)), N, axis=0)); d["py"] = pack(np.repeat(rng.integers(0, 1024, (1, T)), N, axis=0))
    return d
def setup_inputs_line(rng):
    d = setup_inputs(rng)
    d["px"] = pack(rng.integers(0, 1025 - T, (N, 1)) + np.arange(T)); d["py"] = pack(np.repeat(rng.integers(0, 1024, (N, 1)), T, axis=1))
    return d
def setup_inputs_spread(rng):
    d = setup_inputs(rng); d["tb"] = owned(wide(rng, N, 128, 4 * K, cols=4)); return d
def check_inputs(d):
    b = []
    for r in range(N):
        for n in ("px", "py"):
            e = entries(d[n][r])
            if e.min() < 0 or e.max() > 1023: b.append(n)
        t = d["tb"][r].reshape(8, 16, -1).astype(np.float32)
        if any((t[g] != 0).any() for g in range(8) if g not in levels(r)): b.append("tb")
    return b
def addresses(x, y):
    return np.stack([((x >> SH[g]) * A[g] + (y >> SH[g]) * B[g]) & (K - 1) for g in range(8)])
def reference(tb, px, py, w):
    y = np.zeros((N, 128, O * T), np.float32)
    for r in range(N):
        e = addresses(entries(px[r]), entries(py[r])); E = []
        for q in range(N):
            a = np.full((8, T), -1); a[levels(q)] = e[levels(q)]
            E.append(mx_ref.quantize(np.ascontiguousarray(gcols(tb[q], a))))
        for o in range(O):
            W = mx_ref.quantize(np.ascontiguousarray(cut(w[r], o)))
            Z = mx_ref.matmul(W, E[0])
            for q in range(1, N): Z = Z + mx_ref.matmul(W, E[q])
            y[r][:, T * o:T * o + T] = Z
    return {"y": y}

@@ -1,0 +1,278 @@
+from concourse.bass import DstId, RemoteDMATransfer
+from concourse.mybir import dt, AluOpType, ActivationFunctionType
+
+SH = (7, 6, 5, 4, 3, 2, 1, 0)
+A = (1531, 797, 1877, 1129, 619, 1993, 1367, 911)
+B = (1013, 1741, 587, 1459, 1907, 733, 1229, 1667)
+BF, F32, I32, U16, X4, U8 = "bfloat16", "float32", "int32", "uint16", "float8_e4m3fn_x4", "uint8"
+
+SCRATCH = {
+    "st": ("sbuf", [128, 1024], BF),
+    "wn": ("sbuf", [128, 1024], BF),
+    "zt": ("sbuf", [128, 512], BF),
+    "wx": ("sbuf", [128, 2048], BF),
+    "wy": ("sbuf", [128, 2048], BF),
+    "xy": ("sbuf", [128, 16], I32),
+    "pi": ("sbuf", [128, 8], I32), "b0": ("sbuf", [128, 8], I32), "b1": ("sbuf", [128, 1], I32),
+    "kt": ("sbuf", [128, 16], F32), "ke": ("sbuf", [128, 4], F32),
+    "ab": ("sbuf", [128, 32], I32), "un": ("sbuf", [128, 32], I32), "mn": ("sbuf", [128, 32], I32),
+    "an": ("sbuf", [128, 16], I32), "bn": ("sbuf", [128, 16], I32),
+    "off0": ("sbuf", [128, 8], U16), "off1": ("sbuf", [128, 8], U16),
+    "arr": ("sbuf", [128, 64], U16),
+    "e": ("sbuf", [128, 4096], BF),
+    "eq": ("sbuf", [128, 1024], X4), "es": ("sbuf", [128, 1024], U8),
+    "rq": ("sbuf", [128, 1024], X4), "rs": ("sbuf", [128, 1024], U8),
+    "yo": ("sbuf", [128, 1024], F32),
+    "ps": ("psum", [128, 4096], F32),
+}
+for _n in ("s00", "s01", "s10", "s11"):
+    SCRATCH[_n + "q"] = ("sbuf", [128, 512], X4)
+    SCRATCH[_n + "s"] = ("sbuf", [128, 512], U8)
+
+SEMAPHORES = ["v", "io_", "xy", "st", "zt", "zs", "wx", "wy", "fx", "fy", "on0", "on1", "go", "sp", "lo", "yd"]
+SEMAPHORES += ["q00", "q01", "q10", "q11"]
+SEMAPHORES += ["%s%d" % (n, s) for n in ("a", "n", "gs", "gv", "eq", "f") for s in range(8)]
+SEMAPHORES += ["y%d" % o for o in range(4)]
+
+
+def rank_program(g, core, T, topo):
+    r = T.rank_of(core)
+    if r is None:
+        return
+    S = T.sem
+    cores = list(T.cores)
+    Q, F = r // 4, 1 - r // 4
+    copy = ActivationFunctionType.Copy
+    add, mult = AluOpType.add, AluOpType.mult
+    shr, band = AluOpType.arith_shift_right, AluOpType.bitwise_and
+
+    def chip(q):
+        return topo.chip(cores[q])
+
+    def dst(q):
+        rid, pid, _ = topo.addr(cores[q])
+        return DstId(rid=rid, pnc=pid)
+
+    def bits(es):
+        return sum(1 << e for e in es)
+
+    same_chip = [q for q in range(8) if chip(q) == chip(r)]
+    idx = same_chip.index(r)
+    partner = [q for q in same_chip if q != r][0]
+    mates = [q for q in range(4 * Q, 4 * Q + 4) if q not in same_chip]
+    mates = [mates[idx], mates[1 - idx]]
+    far_all = list(range(4 * F, 4 * F + 4))
+    far1 = [q for q in far_all if topo.same_plane(chip(q), chip(r))]
+    far2 = [q for q in far_all if q not in far1]
+    off = topo.engines(core, cores[mates[0]])
+    inner = [e for e in topo.engines(core, cores[partner]) if e not in off]
+    off_mask, in_mask, n_off, n_in = bits(off), bits(inner), len(off), len(inner)
+    half_a, half_b = bits(off[:n_off // 2]), bits(off[n_off // 2:])
+
+    units = [([r], (3,)), ([partner], (3,)), (far2, (3,)), (far1, (3,)), ([mates[0]], (3,)), ([mates[1]], (2, 3))]
+
+    near_rows, far_rows = slice(64 * Q, 64 * Q + 64), slice(64 * F, 64 * F + 64)
+    for k in range(8):
+        h = k // 4
+        g.sync.dma_start(T.xy[16 * k:16 * k + 16, 0:8], T.px[:, 8 * h:8 * h + 8]).then_inc(S.xy, 16)
+        g.scalar.dma_start(T.xy[16 * k:16 * k + 16, 8:16], T.py[:, 8 * h:8 * h + 8]).then_inc(S.xy, 16)
+    g.sync.dma_start(T.st[0:64, :], T.tb[near_rows, :]).then_inc(S.st, 16)
+    g.scalar.dma_start(T.st[64:128, :], T.tb[near_rows, :]).then_inc(S.st, 16)
+    g.sync.dma_start(T.wx[0:64, :], T.w[near_rows, :]).then_inc(S.wx, 16)
+    g.sync.wait_ge(S.zt, 1)
+    for k in (1, 2, 3):
+        g.sync.dma_start(T.wx[64:128, 512 * k:512 * k + 512], T.zt[64:128, :]).then_inc(S.wx, 16)
+    g.sync.wait_ge(S.go, 1)
+    g.sync.dma_start(T.wy[64:128, :], T.w[near_rows, :]).then_inc(S.wy, 16)
+    for k in (2, 3):
+        g.sync.dma_start(T.wy[0:64, 512 * k:512 * k + 512], T.zt[0:64, :]).then_inc(S.wy, 16)
+    g.sync.wait_ge(S["q%d0" % Q], 1)
+    g.sync.dma_start(T.wx[0:64, :], T.w[far_rows, :]).then_inc(S.fx, 16)
+    g.sync.wait_ge(S["q%d1" % Q], 1)
+    g.sync.dma_start(T.wy[64:128, :], T.w[far_rows, :]).then_inc(S.fy, 16)
+
+    lo = [0]
+
+    def send(transfers, n):
+        g.remote_dma_fused(transfers, local_sem=S.lo)
+        lo[0] += n
+
+    def xfer(dests, mask, sem, src, to):
+        return RemoteDMATransfer(dst_ids=[dst(q) for q in dests], dma_engine_mask=mask, remote_sem=sem,
+                                 srcs=[src], dsts=[to for q in dests], alu_op=0)
+
+    g.iota(T.pi[:, 0:8], [[0, 8]], 0, 1).then_inc(S["io_"], 1)
+    slot = T.arr[:, 8 * r:8 * r + 8]
+    own = T["off%d" % Q]
+    g.wait_ge(S["on%d" % F], 1)
+    send([xfer(far2 + far1, off_mask, S["a%d" % r], T["off%d" % F][:, 0:8], slot)], n_off)
+    g.wait_ge(S["on%d" % Q], 1)
+    send([xfer(mates, off_mask, S["a%d" % r], own[:, 0:8], slot),
+          xfer([partner], in_mask, S["a%d" % r], own[:, 0:8], slot)], n_off + n_in)
+    g.sem_inc(S.go)
+
+    def codes(q, mask, plane):
+        a, b = 128 * q, 128 * r
+        if plane:
+            return xfer([q], mask, S["n%d" % r], T.es[:, a:a + 128], T.rs[:, b:b + 128])
+        return xfer([q], mask, S["n%d" % r], T.eq[:, a:a + 128].bitcast(dt.uint8), T.rq[:, b:b + 128].bitcast(dt.uint8))
+
+    for qs, _ in units[1:]:
+        g.wait_ge(S["eq%d" % qs[0]], 1)
+        for plane in (False, True):
+            if len(qs) == 2:
+                send([codes(qs[0], half_a, plane), codes(qs[1], half_b, plane)], n_off)
+            elif qs[0] == partner:
+                send([codes(partner, in_mask, plane)], n_in)
+            else:
+                send([codes(qs[0], off_mask, plane)], n_off)
+    g.wait_ge(S.lo, lo[0])
+
+    def arrivals(q):
+        return 2 * (n_in if q == partner else n_off if q in mates else n_off // 2)
+
+    v = g.vector
+    vn = [0]
+
+    def V(i):
+        i.then_inc(S.v, 1)
+        vn[0] += 1
+
+    def vsync():
+        v.wait_ge(S.v, vn[0])
+
+    v.memset(T.zt[:, :], 0.0).then_inc(S.zt, 1)
+    v.wait_ge(S["io_"], 1)
+    V(v.tensor_scalar(T.b1[:, 0:1], T.pi[:, 0:1], 5, 1, shr, band))
+    V(v.tensor_scalar(T.b0[:, 0:8], T.pi[:, 0:8], 4, 1, shr, band))
+    vsync()
+    c = 2.0 ** -SH[0]
+    V(v.tensor_scalar(T.kt[:, 0:1], T.b1[:, 0:1], 3 * c, c, mult, add))
+    tabs = [(m, s, (A, B)[m][4 * s:4 * s + 4]) for m in range(2) for s in range(2)]
+    for i, (m, s, z) in enumerate(tabs):
+        V(v.tensor_scalar(T.kt[:, 2 * i + 2:2 * i + 3], T.b1[:, 0:1], float(z[3] - z[2] - z[1] + z[0]), float(z[1] - z[0]), mult, add))
+        V(v.tensor_scalar(T.kt[:, 2 * i + 3:2 * i + 4], T.b1[:, 0:1], float(z[2] - z[0]), float(z[0]), mult, add))
+    vsync()
+    V(v.tensor_scalar(T.ke[:, 0:1], T.b0[:, 0:1], T.kt[:, 0:1], T.kt[:, 0:1], mult, add))
+    for i, (m, s, z) in enumerate(tabs):
+        V(v.tensor_scalar(T.ab[:, 16 * m + s:16 * m + 16:2], T.b0[:, 0:8], T.kt[:, 2 * i + 2:2 * i + 3], T.kt[:, 2 * i + 3:2 * i + 4], mult, add))
+    vsync()
+    V(v.tensor_scalar(T.ke[:, 1:2], T.ke[:, 0:1], 0.5, -0.5, mult, add))
+    V(v.tensor_scalar(T.ke[:, 2:3], T.ke[:, 0:1], 16.0, None, mult))
+    V(v.tensor_scalar(T.ke[:, 3:4], T.ke[:, 0:1], 8.0, -0.5, mult, add))
+    v.wait_ge(S.xy, 256)
+    vsync()
+    for s in range(2):
+        V(v.tensor_scalar(T.un[:, s:32:2], T.xy[:, 0:16], T.ke[:, 2 * s:2 * s + 1], T.ke[:, 2 * s + 1:2 * s + 2], mult, add))
+    vsync()
+    V(v.tensor_tensor(T.mn[:, 0:32], T.un[:, 0:32], T.ab[:, 0:32], mult))
+    vsync()
+    V(v.tensor_tensor(T.an[:, 0:16], T.mn[:, 0:16], T.mn[:, 16:32], add))
+    vsync()
+    V(v.tensor_scalar(T.bn[:, 0:16], T.an[:, 0:16], 255, None, band))
+    vsync()
+    for s in (F, Q):
+        v.tensor_copy(T["off%d" % s][:, 0:8], T.bn[:, s:16:2]).then_inc(S["on%d" % s], 1)
+
+    def stat(s, h, sem, n):
+        v.wait_ge(S[sem], n)
+        src = T.wx if h == 0 else T.wy
+        v.quantize_mx(T["s%d%dq" % (s, h)][:, 0:512], T["s%d%ds" % (s, h)][:, 0:512], src[:, 0:2048]).then_inc(S["q%d%d" % (s, h)], 1)
+
+    def wait_lists(queue, qs):
+        for q in qs:
+            if q == r:
+                queue.wait_ge(S["on%d" % Q], 1)
+            else:
+                queue.wait_ge(S["a%d" % q], n_in if q == partner else n_off)
+
+    def gather(call, qs, t, sem, *more):
+        q0, n = min(qs), len(qs)
+        lists = own[:, 0:8] if qs[0] == r else T.arr[:, 8 * q0:8 * (q0 + n)]
+        call(T.e[:, 512 * q0 + t:512 * (q0 + n):4], T.wn[:, 256 * t:256 * t + 256].indirect(lists), *more).then_inc(S["%s%d" % (sem, q0)], 1)
+
+    def vgather(u):
+        qs, ts = units[u]
+        wait_lists(v, qs)
+        for t in ts:
+            gather(v.tensor_copy, qs, t, "gv")
+
+    def pack(u):
+        qs, ts = units[u]
+        q0, n = min(qs), len(qs)
+        v.wait_ge(S["gv%d" % q0], len(ts))
+        v.wait_ge(S["gs%d" % q0], 4 - len(ts))
+        a, b = 128 * q0, 128 * (q0 + n)
+        cq, cs = (T.rq, T.rs) if q0 == r else (T.eq, T.es)
+        v.quantize_mx(cq[:, a:b], cs[:, a:b], T.e[:, 4 * a:4 * b]).then_inc(S["eq%d" % q0], 1)
+
+    v.wait_ge(S.zs, 1)
+    stat(Q, 0, "wx", 64)
+    V(v.memset(T.wy[0:64, 0:1024], 0.0))
+    v.wait_ge(S.sp, 4)
+    vgather(0)
+    vgather(1)
+    pack(0)
+    vsync()
+    stat(Q, 1, "wy", 48)
+    pack(1)
+    vgather(2)
+    stat(F, 0, "fx", 16)
+    pack(2)
+    vgather(3)
+    stat(F, 1, "fy", 16)
+    pack(3)
+    vgather(4)
+    pack(4)
+    vgather(5)
+    pack(5)
+
+    def finish(call, o, h, *more):
+        i = 2 * o + h
+        call(T.yo[:, 128 * i:128 * i + 128], T.ps[:, 512 * i:512 * i + 128], *more).then_inc(S["y%d" % o], 1)
+
+    for o in range(4):
+        v.wait_ge(S["f%d" % (2 * o + 1)], 1)
+        finish(v.tensor_copy, o, 1)
+
+    sc = g.scalar
+    sc.wait_ge(S.zt, 1)
+    sc.activation(T.wx[64:128, 0:512], T.zt[64:128, :], copy).then_inc(S.zs, 1)
+    sc.wait_ge(S.st, 32)
+    for t in range(4):
+        sc.activation(T.wn[:, 256 * t:256 * t + 256], T.st[:, t:1024:4], copy).then_inc(S.sp, 1)
+    sc.wait_ge(S.sp, 4)
+    for qs, ts in units:
+        wait_lists(sc, qs)
+        for t in range(4):
+            if t not in ts:
+                gather(sc.activation, qs, t, "gs", copy)
+    for o in range(4):
+        sc.wait_ge(S["f%d" % (2 * o)], 1)
+        finish(sc.activation, o, 0, copy)
+
+    te = g.tensor
+    order = [q for qs, _ in units for q in qs]
+    for q in order:
+        s = q // 4
+        if q == order[0]:
+            te.wait_ge(S["eq%d" % r], 1)
+            te.wait_ge(S["q%d0" % Q], 1)
+            te.wait_ge(S["q%d1" % Q], 1)
+        else:
+            if q == far2[0]:
+                te.wait_ge(S["q%d0" % F], 1)
+                te.wait_ge(S["q%d1" % F], 1)
+            te.wait_ge(S["n%d" % q], arrivals(q))
+        for i in range(8):
+            o, h = i // 2, i % 2
+            w = slice(128 * o, 128 * o + 128)
+            c = te.matmul_mx(T.ps[:, 512 * i:512 * i + 128], T["s%d%dq" % (s, h)][:, w], T["s%d%ds" % (s, h)][:, w],
+                             T.rq[:, 128 * q:128 * q + 128], T.rs[:, 128 * q:128 * q + 128], q == order[0], q == order[-1])
+            if q == order[-1]:
+                c.then_inc(S["f%d" % i], 1)
+
+    for o in range(4):
+        g.sync.wait_ge(S["y%d" % o], 2)
+        g.sync.dma_start(T.y[:, 256 * o:256 * o + 256], T.yo[:, 256 * o:256 * o + 256]).then_inc(S.yd, 16)
+    g.sync.wait_ge(S.yd, 64)

@@ -6,20 +6,21 @@ A = (1531, 797, 1877, 1129, 619, 1993, 1367, 911)
 B = (1013, 1741, 587, 1459, 1907, 733, 1229, 1667)
 BF, F32, I32, U16, X4, U8 = "bfloat16", "float32", "int32", "uint16", "float8_e4m3fn_x4", "uint8"
 
+RUNS = (((1, 0, 2), (5, 2, 2)), ((0, 0, 1), (3, 1, 2), (7, 3, 1)))
+
 SCRATCH = {
     "st": ("sbuf", [128, 1024], BF),
-    "wn": ("sbuf", [128, 1024], BF),
+    "wn": ("sbuf", [128, 256], BF),
     "zt": ("sbuf", [128, 512], BF),
-    "wx": ("sbuf", [128, 2048], BF),
-    "wy": ("sbuf", [128, 2048], BF),
-    "xy": ("sbuf", [128, 16], I32),
-    "pi": ("sbuf", [128, 8], I32), "b0": ("sbuf", [128, 8], I32), "b1": ("sbuf", [128, 1], I32),
-    "kt": ("sbuf", [128, 16], F32), "ke": ("sbuf", [128, 4], F32),
-    "ab": ("sbuf", [128, 32], I32), "un": ("sbuf", [128, 32], I32), "mn": ("sbuf", [128, 32], I32),
-    "an": ("sbuf", [128, 16], I32), "bn": ("sbuf", [128, 16], I32),
-    "off0": ("sbuf", [128, 8], U16), "off1": ("sbuf", [128, 8], U16),
+    "w0": ("sbuf", [128, 2048], BF),
+    "w1": ("sbuf", [128, 2048], BF),
+    "un": ("sbuf", [128, 2, 64], I32),
+    "ab": ("sbuf", [128, 2, 64], I32), "mn": ("sbuf", [128, 2, 64], I32),
+    "an": ("sbuf", [128, 64], I32), "bn": ("sbuf", [128, 64], I32),
+    "off": ("sbuf", [128, 64], U16),
     "arr": ("sbuf", [128, 64], U16),
-    "e": ("sbuf", [128, 4096], BF),
+    "ga": ("sbuf", [128, 1024], BF),
+    "e": ("sbuf", [128, 2560], BF),
     "eq": ("sbuf", [128, 1024], X4), "es": ("sbuf", [128, 1024], U8),
     "rq": ("sbuf", [128, 1024], X4), "rs": ("sbuf", [128, 1024], U8),
     "yo": ("sbuf", [128, 1024], F32),
@@ -29,9 +30,9 @@ for _n in ("s00", "s01", "s10", "s11"):
     SCRATCH[_n + "q"] = ("sbuf", [128, 512], X4)
     SCRATCH[_n + "s"] = ("sbuf", [128, 512], U8)
 
-SEMAPHORES = ["v", "io_", "xy", "st", "zt", "zs", "wx", "wy", "fx", "fy", "on0", "on1", "go", "sp", "lo", "yd"]
-SEMAPHORES += ["q00", "q01", "q10", "q11"]
-SEMAPHORES += ["%s%d" % (n, s) for n in ("a", "n", "gs", "gv", "eq", "f") for s in range(8)]
+SEMAPHORES = ["va", "vb", "ab", "xy", "st", "zt", "z0", "ze0", "ze1", "ze2", "ze3", "ona", "onb", "sp", "lo", "yd"]
+SEMAPHORES += ["%s%d%d" % (n, s, h) for n in ("q", "l") for s in range(2) for h in range(2)]
+SEMAPHORES += ["%s%d" % (n, s) for n in ("a", "n", "g", "c", "eq", "f") for s in range(8)]
 SEMAPHORES += ["y%d" % o for o in range(4)]
 
 
@@ -41,7 +42,7 @@ def rank_program(g, core, T, topo):
         return
     S = T.sem
     cores = list(T.cores)
-    Q, F = r // 4, 1 - r // 4
+    Q, F, k = r // 4, 1 - r // 4, r % 4
     copy = ActivationFunctionType.Copy
     add, mult = AluOpType.add, AluOpType.mult
     shr, band = AluOpType.arith_shift_right, AluOpType.bitwise_and
@@ -56,221 +57,255 @@ def rank_program(g, core, T, topo):
     def bits(es):
         return sum(1 << e for e in es)
 
-    same_chip = [q for q in range(8) if chip(q) == chip(r)]
-    idx = same_chip.index(r)
-    partner = [q for q in same_chip if q != r][0]
-    mates = [q for q in range(4 * Q, 4 * Q + 4) if q not in same_chip]
-    mates = [mates[idx], mates[1 - idx]]
-    far_all = list(range(4 * F, 4 * F + 4))
-    far1 = [q for q in far_all if topo.same_plane(chip(q), chip(r))]
-    far2 = [q for q in far_all if q not in far1]
-    off = topo.engines(core, cores[mates[0]])
+    def quad(t):
+        return slice(32 * t, 32 * t + 32)
+
+    def group(j, m=1):
+        return slice(16 * j, 16 * (j + m))
+
+    def served(x):
+        rest = sorted((q for q in range(8) if q != x), key=lambda q: topo.die(cores[q]) != topo.die(cores[x]))
+        near = [q for q in rest if chip(q) == chip(x)]
+        mate = [q for q in rest if topo.mates(chip(q), chip(x))]
+        plane = [q for q in rest if topo.same_plane(chip(q), chip(x))]
+        two = [q for q in rest if q not in near + mate + plane]
+        return [[x], mate[:1], mate[1:], two, near, plane[:1], plane[1:]]
+
+    def slot(x, q):
+        return [z for u in served(x) for z in u].index(q)
+
+    units = served(r)
+    partner = units[4][0]
+    place = (2048, 0, 512, 1024, 2048, 0, 512)
+    after = (None, None, None, None, 0, 1, 2)
+    off = topo.engines(core, cores[units[1][0]])
     inner = [e for e in topo.engines(core, cores[partner]) if e not in off]
-    off_mask, in_mask, n_off, n_in = bits(off), bits(inner), len(off), len(inner)
-    half_a, half_b = bits(off[:n_off // 2]), bits(off[n_off // 2:])
+    n = len(off)
+    halves = [off[:n // 2], off[n // 2:]]
+    fourths = [off[i * n // 4:(i + 1) * n // 4] for i in range(4)]
+    for_lists = [None] + halves + fourths[:2] + [inner] + fourths[2:]
+    for_codes = [None, off, off] + halves + [inner, off, off]
+    levels = units[1] + units[2] + units[0] + [q for u in units[3:] for q in u]
+    raw = 8 * levels.index(SH.index(0))
 
-    units = [([r], (3,)), ([partner], (3,)), (far2, (3,)), (far1, (3,)), ([mates[0]], (3,)), ([mates[1]], (2, 3))]
+    for h in range(2):
+        g.sync.dma_start(T.un[group(h), 0, raw:raw + 8], T.px[:, 8 * h:8 * h + 8]).then_inc(S.xy, 16)
+        g.scalar.dma_start(T.un[group(h), 1, raw:raw + 8], T.py[:, 8 * h:8 * h + 8]).then_inc(S.xy, 16)
+    g.sync.dma_start(T.st[group(0), :], T.tb[group(r), :]).then_inc(S.st, 16)
+    g.scalar.dma_start(T.st[group(1), :], T.tb[group(r), :]).then_inc(S.st, 16)
 
-    near_rows, far_rows = slice(64 * Q, 64 * Q + 64), slice(64 * F, 64 * F + 64)
-    for k in range(8):
-        h = k // 4
-        g.sync.dma_start(T.xy[16 * k:16 * k + 16, 0:8], T.px[:, 8 * h:8 * h + 8]).then_inc(S.xy, 16)
-        g.scalar.dma_start(T.xy[16 * k:16 * k + 16, 8:16], T.py[:, 8 * h:8 * h + 8]).then_inc(S.xy, 16)
-    g.sync.dma_start(T.st[0:64, :], T.tb[near_rows, :]).then_inc(S.st, 16)
-    g.scalar.dma_start(T.st[64:128, :], T.tb[near_rows, :]).then_inc(S.st, 16)
-    g.sync.dma_start(T.wx[0:64, :], T.w[near_rows, :]).then_inc(S.wx, 16)
-    g.sync.wait_ge(S.zt, 1)
-    for k in (1, 2, 3):
-        g.sync.dma_start(T.wx[64:128, 512 * k:512 * k + 512], T.zt[64:128, :]).then_inc(S.wx, 16)
-    g.sync.wait_ge(S.go, 1)
-    g.sync.dma_start(T.wy[64:128, :], T.w[near_rows, :]).then_inc(S.wy, 16)
-    for k in (2, 3):
-        g.sync.dma_start(T.wy[0:64, 512 * k:512 * k + 512], T.zt[0:64, :]).then_inc(S.wy, 16)
-    g.sync.wait_ge(S["q%d0" % Q], 1)
-    g.sync.dma_start(T.wx[0:64, :], T.w[far_rows, :]).then_inc(S.fx, 16)
-    g.sync.wait_ge(S["q%d1" % Q], 1)
-    g.sync.dma_start(T.wy[64:128, :], T.w[far_rows, :]).then_inc(S.fy, 16)
+    def load(s, h):
+        for a, b, m in RUNS[h]:
+            g.sync.dma_start(T["w%d" % h][group(a, m), :], T.w[group(4 * s + b, m), :]).then_inc(S["l%d%d" % (s, h)], 16)
+
+    load(Q, 1)
+    g.sync.wait_ge(S.z0, 1)
+    load(Q, 0)
+    for a, _, m in RUNS[0]:
+        g.sync.dma_start(T.w1[group(a, m), :], T.w0[group(RUNS[1][1][0], m), :]).then_inc(S["l%d1" % Q], 16)
+    for h in range(2):
+        g.sync.wait_ge(S["q%d%d" % (Q, h)], 1)
+        load(F, h)
 
     lo = [0]
 
-    def send(transfers, n):
-        g.remote_dma_fused(transfers, local_sem=S.lo)
-        lo[0] += n
+    def send(qs, engines, sem, sides):
+        ts = []
+        for q in qs:
+            es = engines[slot(r, q)]
+            src, to = sides(q)
+            ts.append(RemoteDMATransfer(dst_ids=[dst(q)], dma_engine_mask=bits(es), remote_sem=sem, srcs=[src], dsts=[to], alu_op=0))
+            lo[0] += len(es)
+        g.remote_dma_fused(ts, local_sem=S.lo)
 
-    def xfer(dests, mask, sem, src, to):
-        return RemoteDMATransfer(dst_ids=[dst(q) for q in dests], dma_engine_mask=mask, remote_sem=sem,
-                                 srcs=[src], dsts=[to for q in dests], alu_op=0)
+    def lists(q):
+        a, b = 8 * levels.index(q), 8 * slot(q, r)
+        return T.off[:, a:a + 8], T.arr[:, b:b + 8]
 
-    g.iota(T.pi[:, 0:8], [[0, 8]], 0, 1).then_inc(S["io_"], 1)
-    slot = T.arr[:, 8 * r:8 * r + 8]
-    own = T["off%d" % Q]
-    g.wait_ge(S["on%d" % F], 1)
-    send([xfer(far2 + far1, off_mask, S["a%d" % r], T["off%d" % F][:, 0:8], slot)], n_off)
-    g.wait_ge(S["on%d" % Q], 1)
-    send([xfer(mates, off_mask, S["a%d" % r], own[:, 0:8], slot),
-          xfer([partner], in_mask, S["a%d" % r], own[:, 0:8], slot)], n_off + n_in)
-    g.sem_inc(S.go)
+    def codes(q):
+        a, b = 128 * slot(r, q), 128 * r
+        return T.eq[:, a:a + 128].bitcast(dt.uint8), T.rq[:, b:b + 128].bitcast(dt.uint8)
 
-    def codes(q, mask, plane):
-        a, b = 128 * q, 128 * r
-        if plane:
-            return xfer([q], mask, S["n%d" % r], T.es[:, a:a + 128], T.rs[:, b:b + 128])
-        return xfer([q], mask, S["n%d" % r], T.eq[:, a:a + 128].bitcast(dt.uint8), T.rq[:, b:b + 128].bitcast(dt.uint8))
+    def planes(q):
+        a, b = 128 * slot(r, q), 128 * r
+        return T.es[:, a:a + 128], T.rs[:, b:b + 128]
 
-    for qs, _ in units[1:]:
-        g.wait_ge(S["eq%d" % qs[0]], 1)
-        for plane in (False, True):
-            if len(qs) == 2:
-                send([codes(qs[0], half_a, plane), codes(qs[1], half_b, plane)], n_off)
-            elif qs[0] == partner:
-                send([codes(partner, in_mask, plane)], n_in)
-            else:
-                send([codes(qs[0], off_mask, plane)], n_off)
+    for i, l in enumerate(levels):
+        g.iota(T.ab[0:32, :, 8 * i:8 * i + 8], [[B[l] - A[l], 2], [0, 8]], A[l], 0).then_inc(S.ab, 1)
+    g.wait_ge(S.ona, 4)
+    send(levels[:2], for_lists, S["a%d" % r], lists)
+    g.wait_ge(S.onb, 4)
+    send(levels[3:], for_lists, S["a%d" % r], lists)
+    for u in range(1, 7):
+        g.wait_ge(S["eq%d" % u], 1)
+        send(units[u], for_codes, S["n%d" % r], codes)
+        send(units[u], for_codes, S["n%d" % r], planes)
     g.wait_ge(S.lo, lo[0])
 
-    def arrivals(q):
-        return 2 * (n_in if q == partner else n_off if q in mates else n_off // 2)
+    v, sc = g.vector, g.scalar
+    done = {"a": 0, "b": 0}
+    cols = {"a": slice(0, 16), "b": slice(16, 64)}
 
-    v = g.vector
-    vn = [0]
+    def step(c, call, *args):
+        call(*args).then_inc(S["v" + c], 1)
+        done[c] += 1
 
-    def V(i):
-        i.then_inc(S.v, 1)
-        vn[0] += 1
+    def shifts(c, places):
+        for i in places:
+            if 8 * i != raw:
+                step(c, v.tensor_scalar, T.un[0:32, :, 8 * i:8 * i + 8], T.un[0:32, :, raw:raw + 8], SH[levels[i]], None, shr)
 
-    def vsync():
-        v.wait_ge(S.v, vn[0])
+    def link(c, i):
+        z = cols[c]
+        v.wait_ge(S["v" + c], done[c])
+        if i == 0:
+            step(c, v.tensor_tensor, T.mn[0:32, :, z], T.un[0:32, :, z], T.ab[0:32, :, z], mult)
+        elif i == 1:
+            step(c, v.tensor_tensor, T.an[0:32, z], T.mn[0:32, 0, z], T.mn[0:32, 1, z], add)
+        elif i == 2:
+            step(c, v.tensor_scalar, T.bn[0:32, z], T.an[0:32, z], 255, None, band)
+        else:
+            for t in range(4):
+                v.tensor_copy(T.off[quad(t), z], T.bn[0:32, z]).then_inc(S["on" + c], 1)
 
+    v.memset(T.w0[:, :], 0.0).then_inc(S.z0, 1)
     v.memset(T.zt[:, :], 0.0).then_inc(S.zt, 1)
-    v.wait_ge(S["io_"], 1)
-    V(v.tensor_scalar(T.b1[:, 0:1], T.pi[:, 0:1], 5, 1, shr, band))
-    V(v.tensor_scalar(T.b0[:, 0:8], T.pi[:, 0:8], 4, 1, shr, band))
-    vsync()
-    c = 2.0 ** -SH[0]
-    V(v.tensor_scalar(T.kt[:, 0:1], T.b1[:, 0:1], 3 * c, c, mult, add))
-    tabs = [(m, s, (A, B)[m][4 * s:4 * s + 4]) for m in range(2) for s in range(2)]
-    for i, (m, s, z) in enumerate(tabs):
-        V(v.tensor_scalar(T.kt[:, 2 * i + 2:2 * i + 3], T.b1[:, 0:1], float(z[3] - z[2] - z[1] + z[0]), float(z[1] - z[0]), mult, add))
-        V(v.tensor_scalar(T.kt[:, 2 * i + 3:2 * i + 4], T.b1[:, 0:1], float(z[2] - z[0]), float(z[0]), mult, add))
-    vsync()
-    V(v.tensor_scalar(T.ke[:, 0:1], T.b0[:, 0:1], T.kt[:, 0:1], T.kt[:, 0:1], mult, add))
-    for i, (m, s, z) in enumerate(tabs):
-        V(v.tensor_scalar(T.ab[:, 16 * m + s:16 * m + 16:2], T.b0[:, 0:8], T.kt[:, 2 * i + 2:2 * i + 3], T.kt[:, 2 * i + 3:2 * i + 4], mult, add))
-    vsync()
-    V(v.tensor_scalar(T.ke[:, 1:2], T.ke[:, 0:1], 0.5, -0.5, mult, add))
-    V(v.tensor_scalar(T.ke[:, 2:3], T.ke[:, 0:1], 16.0, None, mult))
-    V(v.tensor_scalar(T.ke[:, 3:4], T.ke[:, 0:1], 8.0, -0.5, mult, add))
-    v.wait_ge(S.xy, 256)
-    vsync()
-    for s in range(2):
-        V(v.tensor_scalar(T.un[:, s:32:2], T.xy[:, 0:16], T.ke[:, 2 * s:2 * s + 1], T.ke[:, 2 * s + 1:2 * s + 2], mult, add))
-    vsync()
-    V(v.tensor_tensor(T.mn[:, 0:32], T.un[:, 0:32], T.ab[:, 0:32], mult))
-    vsync()
-    V(v.tensor_tensor(T.an[:, 0:16], T.mn[:, 0:16], T.mn[:, 16:32], add))
-    vsync()
-    V(v.tensor_scalar(T.bn[:, 0:16], T.an[:, 0:16], 255, None, band))
-    vsync()
-    for s in (F, Q):
-        v.tensor_copy(T["off%d" % s][:, 0:8], T.bn[:, s:16:2]).then_inc(S["on%d" % s], 1)
+    v.wait_ge(S.xy, 64)
+    shifts("a", (0, 1))
+    shifts("b", (2, 3))
+    v.wait_ge(S.ab, 8)
+    link("a", 0)
+    shifts("b", (4, 5))
+    link("a", 1)
+    shifts("b", (6, 7))
+    link("a", 2)
+    link("b", 0)
+    link("a", 3)
+    for i in (1, 2, 3):
+        link("b", i)
 
-    def stat(s, h, sem, n):
-        v.wait_ge(S[sem], n)
-        src = T.wx if h == 0 else T.wy
-        v.quantize_mx(T["s%d%dq" % (s, h)][:, 0:512], T["s%d%ds" % (s, h)][:, 0:512], src[:, 0:2048]).then_inc(S["q%d%d" % (s, h)], 1)
+    def stat(s, h, m):
+        v.wait_ge(S["l%d%d" % (s, h)], m)
+        v.quantize_mx(T["s%d%dq" % (s, h)][:, 0:512], T["s%d%ds" % (s, h)][:, 0:512], T["w%d" % h][:, 0:2048]).then_inc(S["q%d%d" % (s, h)], 1)
 
-    def wait_lists(queue, qs):
-        for q in qs:
+    def gather(u):
+        p, m = slot(r, units[u][0]), len(units[u])
+        for q in units[u]:
             if q == r:
-                queue.wait_ge(S["on%d" % Q], 1)
+                sc.wait_ge(S.onb, 4)
             else:
-                queue.wait_ge(S["a%d" % q], n_in if q == partner else n_off)
+                sc.wait_ge(S["a%d" % q], len(for_lists[slot(q, r)]))
+        ls = T.off[:, 16:24] if u == 0 else T.arr[:, 8 * p:8 * (p + m)]
+        sc.activation(T.ga[:, 128 * p:128 * (p + m)], T.wn[:, 0:256].indirect(ls), copy).then_inc(S["g%d" % u], 1)
 
-    def gather(call, qs, t, sem, *more):
-        q0, n = min(qs), len(qs)
-        lists = own[:, 0:8] if qs[0] == r else T.arr[:, 8 * q0:8 * (q0 + n)]
-        call(T.e[:, 512 * q0 + t:512 * (q0 + n):4], T.wn[:, 256 * t:256 * t + 256].indirect(lists), *more).then_inc(S["%s%d" % (sem, q0)], 1)
-
-    def vgather(u):
-        qs, ts = units[u]
-        wait_lists(v, qs)
+    def spread(on_vector, u, ts):
+        p, m, a = slot(r, units[u][0]), len(units[u]), place[u]
+        queue = v if on_vector else sc
+        if after[u] is None:
+            queue.wait_ge(S["ze%d" % u], 2)
+        else:
+            queue.wait_ge(S["eq%d" % after[u]], 1)
+        queue.wait_ge(S["g%d" % u], 1)
         for t in ts:
-            gather(v.tensor_copy, qs, t, "gv")
+            to, src = T.e[quad(k), a + t:a + 512 * m:4], T.ga[quad(t), 128 * p:128 * (p + m)]
+            (v.tensor_copy(to, src) if on_vector else sc.activation(to, src, copy)).then_inc(S["c%d" % u], 1)
 
     def pack(u):
-        qs, ts = units[u]
-        q0, n = min(qs), len(qs)
-        v.wait_ge(S["gv%d" % q0], len(ts))
-        v.wait_ge(S["gs%d" % q0], 4 - len(ts))
-        a, b = 128 * q0, 128 * (q0 + n)
-        cq, cs = (T.rq, T.rs) if q0 == r else (T.eq, T.es)
-        v.quantize_mx(cq[:, a:b], cs[:, a:b], T.e[:, 4 * a:4 * b]).then_inc(S["eq%d" % q0], 1)
+        p, m, a = slot(r, units[u][0]), len(units[u]), place[u]
+        v.wait_ge(S["c%d" % u], 4)
+        cq, cs, c = (T.rq, T.rs, r) if u == 0 else (T.eq, T.es, p)
+        c = slice(128 * c, 128 * (c + m))
+        v.quantize_mx(cq[:, c], cs[:, c], T.e[:, a:a + 512 * m]).then_inc(S["eq%d" % u], 1)
 
-    v.wait_ge(S.zs, 1)
-    stat(Q, 0, "wx", 64)
-    V(v.memset(T.wy[0:64, 0:1024], 0.0))
-    v.wait_ge(S.sp, 4)
-    vgather(0)
-    vgather(1)
+    stat(Q, 0, 32)
+    stat(Q, 1, 80)
+    v.memset(T.e[:, 1024:2048], 0.0).then_inc(S.ze3, 2)
+    spread(True, 0, (0, 1, 2, 3))
     pack(0)
-    vsync()
-    stat(Q, 1, "wy", 48)
+    spread(True, 1, (0, 1, 2, 3))
     pack(1)
-    vgather(2)
-    stat(F, 0, "fx", 16)
+    spread(True, 2, (0, 1, 2, 3))
     pack(2)
-    vgather(3)
-    stat(F, 1, "fy", 16)
+    spread(True, 3, (0, 1, 2))
+    spread(True, 4, (0, 1))
     pack(3)
-    vgather(4)
+    spread(True, 4, (2, 3))
+    spread(True, 5, (0, 1, 2))
     pack(4)
-    vgather(5)
     pack(5)
+    spread(True, 6, (0, 1))
+    stat(F, 0, 32)
+    pack(6)
+    stat(F, 1, 48)
+
+    def zero(a, sem, m):
+        sc.activation(T.e[:, a:a + 512], T.zt[:, :], copy).then_inc(sem, m)
+
+    sc.wait_ge(S.zt, 1)
+    zero(2048, S.ze0, 2)
+    sc.wait_ge(S.st, 32)
+    for t in range(4):
+        sc.activation(T.wn[quad(t), :], T.st[0:32, t:1024:4], copy).then_inc(S.sp, 1)
+    zero(0, S.ze1, 2)
+    sc.wait_ge(S.sp, 4)
+    gather(0)
+    zero(512, S.ze2, 2)
+    for u in range(1, 5):
+        gather(u)
+    spread(False, 3, (3,))
+    gather(5)
+    gather(6)
+    spread(False, 5, (3,))
+    spread(False, 6, (3, 2))
 
     def finish(call, o, h, *more):
         i = 2 * o + h
         call(T.yo[:, 128 * i:128 * i + 128], T.ps[:, 512 * i:512 * i + 128], *more).then_inc(S["y%d" % o], 1)
 
     for o in range(4):
+        sc.wait_ge(S["f%d" % (2 * o)], 1)
+        finish(sc.activation, o, 0, copy)
         v.wait_ge(S["f%d" % (2 * o + 1)], 1)
         finish(v.tensor_copy, o, 1)
 
-    sc = g.scalar
-    sc.wait_ge(S.zt, 1)
-    sc.activation(T.wx[64:128, 0:512], T.zt[64:128, :], copy).then_inc(S.zs, 1)
-    sc.wait_ge(S.st, 32)
-    for t in range(4):
-        sc.activation(T.wn[:, 256 * t:256 * t + 256], T.st[:, t:1024:4], copy).then_inc(S.sp, 1)
-    sc.wait_ge(S.sp, 4)
-    for qs, ts in units:
-        wait_lists(sc, qs)
-        for t in range(4):
-            if t not in ts:
-                gather(sc.activation, qs, t, "gs", copy)
-    for o in range(4):
-        sc.wait_ge(S["f%d" % (2 * o)], 1)
-        finish(sc.activation, o, 0, copy)
-
     te = g.tensor
-    order = [q for qs, _ in units for q in qs]
-    for q in order:
-        s = q // 4
-        if q == order[0]:
-            te.wait_ge(S["eq%d" % r], 1)
-            te.wait_ge(S["q%d0" % Q], 1)
-            te.wait_ge(S["q%d1" % Q], 1)
-        else:
-            if q == far2[0]:
-                te.wait_ge(S["q%d0" % F], 1)
-                te.wait_ge(S["q%d1" % F], 1)
-            te.wait_ge(S["n%d" % q], arrivals(q))
-        for i in range(8):
-            o, h = i // 2, i % 2
-            w = slice(128 * o, 128 * o + 128)
-            c = te.matmul_mx(T.ps[:, 512 * i:512 * i + 128], T["s%d%dq" % (s, h)][:, w], T["s%d%ds" % (s, h)][:, w],
-                             T.rq[:, 128 * q:128 * q + 128], T.rs[:, 128 * q:128 * q + 128], q == order[0], q == order[-1])
-            if q == order[-1]:
-                c.then_inc(S["f%d" % i], 1)
+    last = units[6]
+
+    def product(q, o, b):
+        i, w, s = 2 * o + (q + b + 1) % 2, slice(128 * o, 128 * o + 128), "s%d%d" % (q // 4, b)
+        c = te.matmul_mx(T.ps[:, 512 * i:512 * i + 128], T[s + "q"][:, w], T[s + "s"][:, w],
+                         T.rq[:, 128 * q:128 * q + 128], T.rs[:, 128 * q:128 * q + 128], q == r, q == last[-1])
+        if q == last[-1]:
+            c.then_inc(S["f%d" % i], 1)
+
+    def arrived(qs):
+        for q in qs:
+            te.wait_ge(S["n%d" % q], 2 * len(for_codes[slot(q, r)]))
+
+    def products(qs, hs):
+        for q in qs:
+            for h in hs:
+                for o in range(4):
+                    product(q, o, h)
+
+    te.wait_ge(S.eq0, 1)
+    for h in range(2):
+        te.wait_ge(S["q%d%d" % (Q, h)], 1)
+        products([r], [h])
+    for u in (1, 2, 4):
+        arrived(units[u])
+        products(units[u], [0, 1])
+    arrived(units[3])
+    for h in range(2):
+        te.wait_ge(S["q%d%d" % (F, h)], 1)
+        products(units[3], [h])
+    arrived(units[5])
+    products(units[5], [0, 1])
+    arrived(last)
+    for o in range(4):
+        for h in range(2):
+            for q in last:
+                product(q, o, (q + h + 1) % 2)
 
     for o in range(4):
         g.sync.wait_ge(S["y%d" % o], 2)

@@ -11,16 +11,15 @@ RUNS = (((1, 0, 2), (5, 2, 2)), ((0, 0, 1), (3, 1, 2), (7, 3, 1)))
 SCRATCH = {
     "st": ("sbuf", [128, 1024], BF),
     "wn": ("sbuf", [128, 256], BF),
-    "zt": ("sbuf", [128, 512], BF),
-    "w0": ("sbuf", [128, 2048], BF),
-    "w1": ("sbuf", [128, 2048], BF),
-    "un": ("sbuf", [128, 2, 64], I32),
-    "ab": ("sbuf", [128, 2, 64], I32), "mn": ("sbuf", [128, 2, 64], I32),
+    "w0": ("sbuf", [128, 2048], BF), "w1": ("sbuf", [128, 2048], BF),
+    "xy": ("sbuf", [128, 8], I32),
+    "xr": ("sbuf", [128, 8], I32),
+    "un": ("sbuf", [128, 64], I32), "ab": ("sbuf", [128, 64], I32), "mn": ("sbuf", [128, 2, 64], I32),
     "an": ("sbuf", [128, 64], I32), "bn": ("sbuf", [128, 64], I32),
     "off": ("sbuf", [128, 64], U16),
     "arr": ("sbuf", [128, 64], U16),
     "ga": ("sbuf", [128, 1024], BF),
-    "e": ("sbuf", [128, 2560], BF),
+    "e": ("sbuf", [128, 1536], BF),
     "eq": ("sbuf", [128, 1024], X4), "es": ("sbuf", [128, 1024], U8),
     "rq": ("sbuf", [128, 1024], X4), "rs": ("sbuf", [128, 1024], U8),
     "yo": ("sbuf", [128, 1024], F32),
@@ -30,7 +29,8 @@ for _n in ("s00", "s01", "s10", "s11"):
     SCRATCH[_n + "q"] = ("sbuf", [128, 512], X4)
     SCRATCH[_n + "s"] = ("sbuf", [128, 512], U8)
 
-SEMAPHORES = ["va", "vb", "ab", "xy", "st", "zt", "z0", "ze0", "ze1", "ze2", "ze3", "ona", "onb", "sp", "lo", "yd"]
+SEMAPHORES = ["xy", "xf", "xr", "st", "z0", "ze0", "ze2", "sp", "lo", "yd"]
+SEMAPHORES += ["%s%s" % (n, c) for n in ("v", "on", "ab") for c in "abc"]
 SEMAPHORES += ["%s%d%d" % (n, s, h) for n in ("q", "l") for s in range(2) for h in range(2)]
 SEMAPHORES += ["%s%d" % (n, s) for n in ("a", "n", "g", "c", "eq", "f") for s in range(8)]
 SEMAPHORES += ["y%d" % o for o in range(4)]
@@ -69,28 +69,24 @@ def rank_program(g, core, T, topo):
         mate = [q for q in rest if topo.mates(chip(q), chip(x))]
         plane = [q for q in rest if topo.same_plane(chip(q), chip(x))]
         two = [q for q in rest if q not in near + mate + plane]
-        return [[x], mate[:1], mate[1:], two, near, plane[:1], plane[1:]]
+        return [x] + mate + two[:1] + near + two[1:] + plane
 
     def slot(x, q):
-        return [z for u in served(x) for z in u].index(q)
+        return served(x).index(q)
 
     units = served(r)
-    partner = units[4][0]
-    place = (2048, 0, 512, 1024, 2048, 0, 512)
-    after = (None, None, None, None, 0, 1, 2)
-    off = topo.engines(core, cores[units[1][0]])
-    inner = [e for e in topo.engines(core, cores[partner]) if e not in off]
-    n = len(off)
-    halves = [off[:n // 2], off[n // 2:]]
-    fourths = [off[i * n // 4:(i + 1) * n // 4] for i in range(4)]
-    for_lists = [None] + halves + fourths[:2] + [inner] + fourths[2:]
-    for_codes = [None, off, off] + halves + [inner, off, off]
-    levels = units[1] + units[2] + units[0] + [q for u in units[3:] for q in u]
-    raw = 8 * levels.index(SH.index(0))
+    partner = units[4]
+    off = topo.engines(core, cores[units[1]])
+    every = topo.engines(core, cores[partner])
+    inner = [e for e in every if e not in off]
+    halves = [off[:len(off) // 2], off[len(off) // 2:]]
+    for_lists = [None] + halves + [halves[0], every, halves[1]] + halves
+    for_codes = [None, off, off, off, inner, off, off, off]
+    levels = units[1:4] + units[5:] + [r, r]
 
     for h in range(2):
-        g.sync.dma_start(T.un[group(h), 0, raw:raw + 8], T.px[:, 8 * h:8 * h + 8]).then_inc(S.xy, 16)
-        g.scalar.dma_start(T.un[group(h), 1, raw:raw + 8], T.py[:, 8 * h:8 * h + 8]).then_inc(S.xy, 16)
+        g.sync.dma_start(T.xy[group(h), :], T.px[:, 8 * h:8 * h + 8]).then_inc(S.xy, 16)
+        g.scalar.dma_start(T.xy[group(2 + h), :], T.py[:, 8 * h:8 * h + 8]).then_inc(S.xy, 16)
     g.sync.dma_start(T.st[group(0), :], T.tb[group(r), :]).then_inc(S.st, 16)
     g.scalar.dma_start(T.st[group(1), :], T.tb[group(r), :]).then_inc(S.st, 16)
 
@@ -130,36 +126,43 @@ def rank_program(g, core, T, topo):
         a, b = 128 * slot(r, q), 128 * r
         return T.es[:, a:a + 128], T.rs[:, b:b + 128]
 
-    for i, l in enumerate(levels):
-        g.iota(T.ab[0:32, :, 8 * i:8 * i + 8], [[B[l] - A[l], 2], [0, 8]], A[l], 0).then_inc(S.ab, 1)
+    for i in range(0, 8, 2):
+        for j, z in enumerate((A, B)):
+            a, b = z[levels[i]], z[levels[i + 1]]
+            g.iota(T.ab[quad(j), 8 * i:8 * i + 16], [[b - a, 2], [0, 8]], a, 0).then_inc(S.aba if i == 0 else S.abb, 1)
+    g.wait_ge(S.xf, 1)
+    g.wait_ge(S.xy, 64)
+    send([partner], for_lists, S.xr, lambda q: (T.xy[:, :], T.xr[:, :]))
     g.wait_ge(S.ona, 4)
-    send(levels[:2], for_lists, S["a%d" % r], lists)
+    send(levels[0:2], for_lists, S["a%d" % r], lists)
     g.wait_ge(S.onb, 4)
-    send(levels[3:], for_lists, S["a%d" % r], lists)
-    for u in range(1, 7):
-        g.wait_ge(S["eq%d" % u], 1)
-        send(units[u], for_codes, S["n%d" % r], codes)
-        send(units[u], for_codes, S["n%d" % r], planes)
+    send(levels[2:4], for_lists, S["a%d" % r], lists)
+    send(levels[4:6], for_lists, S["a%d" % r], lists)
+    for us in ([1], [2], [3], [4, 5], [6], [7]):
+        for u in us:
+            g.wait_ge(S["eq%d" % u], 1)
+        send([units[u] for u in us], for_codes, S["n%d" % r], codes)
+        send([units[u] for u in us], for_codes, S["n%d" % r], planes)
     g.wait_ge(S.lo, lo[0])
 
     v, sc = g.vector, g.scalar
-    done = {"a": 0, "b": 0}
-    cols = {"a": slice(0, 16), "b": slice(16, 64)}
+    done = {"a": 0, "b": 0, "c": 0}
+    cols = {"a": slice(0, 16), "b": slice(16, 56), "c": slice(56, 64)}
 
     def step(c, call, *args):
         call(*args).then_inc(S["v" + c], 1)
         done[c] += 1
 
-    def shifts(c, places):
+    def shifts(c, places, src):
         for i in places:
-            if 8 * i != raw:
-                step(c, v.tensor_scalar, T.un[0:32, :, 8 * i:8 * i + 8], T.un[0:32, :, raw:raw + 8], SH[levels[i]], None, shr)
+            step(c, v.tensor_scalar, T.un[0:64, 8 * i:8 * i + 8], src[0:64, :], SH[levels[i]], None, shr)
 
     def link(c, i):
         z = cols[c]
         v.wait_ge(S["v" + c], done[c])
         if i == 0:
-            step(c, v.tensor_tensor, T.mn[0:32, :, z], T.un[0:32, :, z], T.ab[0:32, :, z], mult)
+            for j in range(2):
+                step(c, v.tensor_tensor, T.mn[0:32, j, z], T.un[quad(j), z], T.ab[quad(j), z], mult)
         elif i == 1:
             step(c, v.tensor_tensor, T.an[0:32, z], T.mn[0:32, 0, z], T.mn[0:32, 1, z], add)
         elif i == 2:
@@ -168,16 +171,18 @@ def rank_program(g, core, T, topo):
             for t in range(4):
                 v.tensor_copy(T.off[quad(t), z], T.bn[0:32, z]).then_inc(S["on" + c], 1)
 
+    v.memset(T.xy[64:128, :], 0).then_inc(S.xf, 1)
     v.memset(T.w0[:, :], 0.0).then_inc(S.z0, 1)
-    v.memset(T.zt[:, :], 0.0).then_inc(S.zt, 1)
+    v.memset(T.e[:, 0:1024], 0.0).then_inc(S.ze0, 1)
     v.wait_ge(S.xy, 64)
-    shifts("a", (0, 1))
-    shifts("b", (2, 3))
-    v.wait_ge(S.ab, 8)
+    shifts("a", (0, 1), T.xy)
+    shifts("b", (2, 3), T.xy)
+    v.wait_ge(S.aba, 2)
     link("a", 0)
-    shifts("b", (4, 5))
+    shifts("b", (4, 5), T.xy)
     link("a", 1)
-    shifts("b", (6, 7))
+    shifts("b", (6,), T.xy)
+    v.wait_ge(S.abb, 6)
     link("a", 2)
     link("b", 0)
     link("a", 3)
@@ -189,74 +194,77 @@ def rank_program(g, core, T, topo):
         v.quantize_mx(T["s%d%dq" % (s, h)][:, 0:512], T["s%d%ds" % (s, h)][:, 0:512], T["w%d" % h][:, 0:2048]).then_inc(S["q%d%d" % (s, h)], 1)
 
     def gather(u):
-        p, m = slot(r, units[u][0]), len(units[u])
-        for q in units[u]:
-            if q == r:
-                sc.wait_ge(S.onb, 4)
-            else:
-                sc.wait_ge(S["a%d" % q], len(for_lists[slot(q, r)]))
-        ls = T.off[:, 16:24] if u == 0 else T.arr[:, 8 * p:8 * (p + m)]
-        sc.activation(T.ga[:, 128 * p:128 * (p + m)], T.wn[:, 0:256].indirect(ls), copy).then_inc(S["g%d" % u], 1)
+        if u in (0, 4):
+            sc.wait_ge(S.onb if u == 0 else S.onc, 4)
+            ls = T.off[:, 48:56] if u == 0 else T.off[:, 56:64]
+        else:
+            sc.wait_ge(S["a%d" % units[u]], len(for_lists[slot(units[u], r)]))
+            ls = T.arr[:, 8 * u:8 * u + 8]
+        sc.activation(T.ga[:, 128 * u:128 * u + 128], T.wn[:, 0:256].indirect(ls), copy).then_inc(S["g%d" % u], 1)
 
     def spread(on_vector, u, ts):
-        p, m, a = slot(r, units[u][0]), len(units[u]), place[u]
-        queue = v if on_vector else sc
-        if after[u] is None:
-            queue.wait_ge(S["ze%d" % u], 2)
+        a, queue = 512 * (u % 3), v if on_vector else sc
+        if u < 3:
+            queue.wait_ge(S.ze2, 1)
         else:
-            queue.wait_ge(S["eq%d" % after[u]], 1)
+            queue.wait_ge(S["eq%d" % (u - 3)], 1)
         queue.wait_ge(S["g%d" % u], 1)
         for t in ts:
-            to, src = T.e[quad(k), a + t:a + 512 * m:4], T.ga[quad(t), 128 * p:128 * (p + m)]
+            to, src = T.e[quad(k), a + t:a + 512:4], T.ga[quad(t), 128 * u:128 * u + 128]
             (v.tensor_copy(to, src) if on_vector else sc.activation(to, src, copy)).then_inc(S["c%d" % u], 1)
 
     def pack(u):
-        p, m, a = slot(r, units[u][0]), len(units[u]), place[u]
+        a = 512 * (u % 3)
         v.wait_ge(S["c%d" % u], 4)
-        cq, cs, c = (T.rq, T.rs, r) if u == 0 else (T.eq, T.es, p)
-        c = slice(128 * c, 128 * (c + m))
-        v.quantize_mx(cq[:, c], cs[:, c], T.e[:, a:a + 512 * m]).then_inc(S["eq%d" % u], 1)
+        cq, cs, c = (T.rq, T.rs, r) if u == 0 else (T.eq, T.es, u)
+        v.quantize_mx(cq[:, 128 * c:128 * c + 128], cs[:, 128 * c:128 * c + 128], T.e[:, a:a + 512]).then_inc(S["eq%d" % u], 1)
 
     stat(Q, 0, 32)
     stat(Q, 1, 80)
-    v.memset(T.e[:, 1024:2048], 0.0).then_inc(S.ze3, 2)
-    spread(True, 0, (0, 1, 2, 3))
+    v.wait_ge(S.xr, len(every))
+    shifts("c", (7,), T.xr)
+    spread(True, 0, (0, 1, 2))
+    link("c", 0)
     pack(0)
+    link("c", 1)
     spread(True, 1, (0, 1, 2, 3))
+    link("c", 2)
     pack(1)
     spread(True, 2, (0, 1, 2, 3))
+    link("c", 3)
     pack(2)
     spread(True, 3, (0, 1, 2))
-    spread(True, 4, (0, 1))
+    spread(True, 5, (0, 1))
     pack(3)
-    spread(True, 4, (2, 3))
-    spread(True, 5, (0, 1, 2))
-    pack(4)
+    spread(True, 5, (2,))
+    spread(True, 4, (0, 1, 2, 3))
     pack(5)
     spread(True, 6, (0, 1))
-    stat(F, 0, 32)
+    pack(4)
+    spread(True, 6, (2,))
+    spread(True, 7, (0, 1))
     pack(6)
+    stat(F, 0, 32)
+    pack(7)
     stat(F, 1, 48)
 
-    def zero(a, sem, m):
-        sc.activation(T.e[:, a:a + 512], T.zt[:, :], copy).then_inc(sem, m)
-
-    sc.wait_ge(S.zt, 1)
-    zero(2048, S.ze0, 2)
+    sc.wait_ge(S.ze0, 1)
+    sc.activation(T.e[:, 1024:1536], T.e[:, 0:512], copy).then_inc(S.ze2, 1)
     sc.wait_ge(S.st, 32)
     for t in range(4):
         sc.activation(T.wn[quad(t), :], T.st[0:32, t:1024:4], copy).then_inc(S.sp, 1)
-    zero(0, S.ze1, 2)
     sc.wait_ge(S.sp, 4)
     gather(0)
-    zero(512, S.ze2, 2)
-    for u in range(1, 5):
+    spread(False, 0, (3,))
+    for u in (1, 2, 3, 5):
         gather(u)
     spread(False, 3, (3,))
-    gather(5)
     gather(6)
+    gather(4)
     spread(False, 5, (3,))
-    spread(False, 6, (3, 2))
+    gather(7)
+    spread(False, 6, (3,))
+    spread(False, 7, (3, 2))
 
     def finish(call, o, h, *more):
         i = 2 * o + h
@@ -269,43 +277,43 @@ def rank_program(g, core, T, topo):
         finish(v.tensor_copy, o, 1)
 
     te = g.tensor
-    last = units[6]
+    last = units[7]
 
     def product(q, o, b):
         i, w, s = 2 * o + (q + b + 1) % 2, slice(128 * o, 128 * o + 128), "s%d%d" % (q // 4, b)
         c = te.matmul_mx(T.ps[:, 512 * i:512 * i + 128], T[s + "q"][:, w], T[s + "s"][:, w],
-                         T.rq[:, 128 * q:128 * q + 128], T.rs[:, 128 * q:128 * q + 128], q == r, q == last[-1])
-        if q == last[-1]:
+                         T.rq[:, 128 * q:128 * q + 128], T.rs[:, 128 * q:128 * q + 128], q == r, q == last)
+        if q == last:
             c.then_inc(S["f%d" % i], 1)
 
-    def arrived(qs):
-        for q in qs:
-            te.wait_ge(S["n%d" % q], 2 * len(for_codes[slot(q, r)]))
+    def arrived(q):
+        te.wait_ge(S["n%d" % q], 2 * len(for_codes[slot(q, r)]))
 
-    def products(qs, hs):
-        for q in qs:
-            for h in hs:
-                for o in range(4):
-                    product(q, o, h)
+    def products(q, bs):
+        for b in bs:
+            for o in range(4):
+                product(q, o, b)
 
     te.wait_ge(S.eq0, 1)
-    for h in range(2):
-        te.wait_ge(S["q%d%d" % (Q, h)], 1)
-        products([r], [h])
-    for u in (1, 2, 4):
-        arrived(units[u])
-        products(units[u], [0, 1])
-    arrived(units[3])
-    for h in range(2):
-        te.wait_ge(S["q%d%d" % (F, h)], 1)
-        products(units[3], [h])
-    arrived(units[5])
-    products(units[5], [0, 1])
+    for b in range(2):
+        te.wait_ge(S["q%d%d" % (Q, b)], 1)
+        products(r, [b])
+    for q in units[1:3] + [partner]:
+        arrived(q)
+        products(q, [0, 1])
+    te.wait_ge(S["q%d0" % F], 1)
+    for q in (units[3], units[5]):
+        arrived(q)
+        products(q, [0])
+    te.wait_ge(S["q%d1" % F], 1)
+    for q in (units[3], units[5]):
+        products(q, [1])
+    arrived(units[6])
+    products(units[6], [0, 1])
     arrived(last)
     for o in range(4):
         for h in range(2):
-            for q in last:
-                product(q, o, (q + h + 1) % 2)
+            product(last, o, (last + h + 1) % 2)
 
     for o in range(4):
         g.sync.wait_ge(S["y%d" % o], 2)

from concourse.bass import DstId, RemoteDMATransfer
from concourse.mybir import dt, AluOpType, ActivationFunctionType

SH = (7, 6, 5, 4, 3, 2, 1, 0)
A = (1531, 797, 1877, 1129, 619, 1993, 1367, 911)
B = (1013, 1741, 587, 1459, 1907, 733, 1229, 1667)
BF, F32, I32, U16, X4, U8 = "bfloat16", "float32", "int32", "uint16", "float8_e4m3fn_x4", "uint8"

RUNS = (((1, 0, 2), (5, 2, 2)), ((0, 0, 1), (3, 1, 2), (7, 3, 1)))

SCRATCH = {
    "st": ("sbuf", [128, 1024], BF),
    "wn": ("sbuf", [128, 256], BF),
    "w0": ("sbuf", [128, 2048], BF), "w1": ("sbuf", [128, 2048], BF),
    "xy": ("sbuf", [128, 8], I32),
    "xr": ("sbuf", [128, 8], I32),
    "un": ("sbuf", [128, 64], I32), "ab": ("sbuf", [128, 64], I32), "mn": ("sbuf", [128, 2, 64], I32),
    "an": ("sbuf", [128, 64], I32), "bn": ("sbuf", [128, 64], I32),
    "off": ("sbuf", [128, 64], U16),
    "arr": ("sbuf", [128, 64], U16),
    "ga": ("sbuf", [128, 1024], BF),
    "e": ("sbuf", [128, 1536], BF),
    "eq": ("sbuf", [128, 1024], X4), "es": ("sbuf", [128, 1024], U8),
    "rq": ("sbuf", [128, 1024], X4), "rs": ("sbuf", [128, 1024], U8),
    "yo": ("sbuf", [128, 1024], F32),
    "ps": ("psum", [128, 4096], F32),
}
for _n in ("s00", "s01", "s10", "s11"):
    SCRATCH[_n + "q"] = ("sbuf", [128, 512], X4)
    SCRATCH[_n + "s"] = ("sbuf", [128, 512], U8)

SEMAPHORES = ["xy", "xf", "xr", "st", "z0", "ze0", "ze2", "sp", "lo", "yd"]
SEMAPHORES += ["%s%s" % (n, c) for n in ("v", "on", "ab") for c in "abc"]
SEMAPHORES += ["%s%d%d" % (n, s, h) for n in ("q", "l") for s in range(2) for h in range(2)]
SEMAPHORES += ["%s%d" % (n, s) for n in ("a", "n", "g", "c", "eq", "f") for s in range(8)]
SEMAPHORES += ["y%d" % o for o in range(4)]


def rank_program(g, core, T, topo):
    r = T.rank_of(core)
    if r is None:
        return
    S = T.sem
    cores = list(T.cores)
    Q, F, k = r // 4, 1 - r // 4, r % 4
    copy = ActivationFunctionType.Copy
    add, mult = AluOpType.add, AluOpType.mult
    shr, band = AluOpType.arith_shift_right, AluOpType.bitwise_and

    def chip(q):
        return topo.chip(cores[q])

    def dst(q):
        rid, pid, _ = topo.addr(cores[q])
        return DstId(rid=rid, pnc=pid)

    def bits(es):
        return sum(1 << e for e in es)

    def quad(t):
        return slice(32 * t, 32 * t + 32)

    def group(j, m=1):
        return slice(16 * j, 16 * (j + m))

    def served(x):
        rest = sorted((q for q in range(8) if q != x), key=lambda q: topo.die(cores[q]) != topo.die(cores[x]))
        near = [q for q in rest if chip(q) == chip(x)]
        mate = [q for q in rest if topo.mates(chip(q), chip(x))]
        plane = [q for q in rest if topo.same_plane(chip(q), chip(x))]
        two = [q for q in rest if q not in near + mate + plane]
        return [x] + mate + two[:1] + near + two[1:] + plane

    def slot(x, q):
        return served(x).index(q)

    units = served(r)
    partner = units[4]
    off = topo.engines(core, cores[units[1]])
    every = topo.engines(core, cores[partner])
    inner = [e for e in every if e not in off]
    halves = [off[:len(off) // 2], off[len(off) // 2:]]
    for_lists = [None] + halves + [halves[0], every, halves[1]] + halves
    for_codes = [None, off, off, off, inner, off, off, off]
    levels = units[1:4] + units[5:] + [r, r]

    for h in range(2):
        g.sync.dma_start(T.xy[group(h), :], T.px[:, 8 * h:8 * h + 8]).then_inc(S.xy, 16)
        g.scalar.dma_start(T.xy[group(2 + h), :], T.py[:, 8 * h:8 * h + 8]).then_inc(S.xy, 16)
    g.sync.dma_start(T.st[group(0), :], T.tb[group(r), :]).then_inc(S.st, 16)
    g.scalar.dma_start(T.st[group(1), :], T.tb[group(r), :]).then_inc(S.st, 16)

    def load(s, h):
        for a, b, m in RUNS[h]:
            g.sync.dma_start(T["w%d" % h][group(a, m), :], T.w[group(4 * s + b, m), :]).then_inc(S["l%d%d" % (s, h)], 16)

    load(Q, 1)
    g.sync.wait_ge(S.z0, 1)
    load(Q, 0)
    for a, _, m in RUNS[0]:
        g.sync.dma_start(T.w1[group(a, m), :], T.w0[group(RUNS[1][1][0], m), :]).then_inc(S["l%d1" % Q], 16)
    for h in range(2):
        g.sync.wait_ge(S["q%d%d" % (Q, h)], 1)
        load(F, h)

    lo = [0]

    def send(qs, engines, sem, sides):
        ts = []
        for q in qs:
            es = engines[slot(r, q)]
            src, to = sides(q)
            ts.append(RemoteDMATransfer(dst_ids=[dst(q)], dma_engine_mask=bits(es), remote_sem=sem, srcs=[src], dsts=[to], alu_op=0))
            lo[0] += len(es)
        g.remote_dma_fused(ts, local_sem=S.lo)

    def lists(q):
        a, b = 8 * levels.index(q), 8 * slot(q, r)
        return T.off[:, a:a + 8], T.arr[:, b:b + 8]

    def codes(q):
        a, b = 128 * slot(r, q), 128 * r
        return T.eq[:, a:a + 128].bitcast(dt.uint8), T.rq[:, b:b + 128].bitcast(dt.uint8)

    def planes(q):
        a, b = 128 * slot(r, q), 128 * r
        return T.es[:, a:a + 128], T.rs[:, b:b + 128]

    for i in range(0, 8, 2):
        for j, z in enumerate((A, B)):
            a, b = z[levels[i]], z[levels[i + 1]]
            g.iota(T.ab[quad(j), 8 * i:8 * i + 16], [[b - a, 2], [0, 8]], a, 0).then_inc(S.aba if i == 0 else S.abb, 1)
    g.wait_ge(S.xf, 1)
    g.wait_ge(S.xy, 64)
    send([partner], for_lists, S.xr, lambda q: (T.xy[:, :], T.xr[:, :]))
    g.wait_ge(S.ona, 4)
    send(levels[0:2], for_lists, S["a%d" % r], lists)
    g.wait_ge(S.onb, 4)
    send(levels[2:4], for_lists, S["a%d" % r], lists)
    send(levels[4:6], for_lists, S["a%d" % r], lists)
    for us in ([1], [2], [3], [4, 5], [6], [7]):
        for u in us:
            g.wait_ge(S["eq%d" % u], 1)
        send([units[u] for u in us], for_codes, S["n%d" % r], codes)
        send([units[u] for u in us], for_codes, S["n%d" % r], planes)
    g.wait_ge(S.lo, lo[0])

    v, sc = g.vector, g.scalar
    done = {"a": 0, "b": 0, "c": 0}
    cols = {"a": slice(0, 16), "b": slice(16, 56), "c": slice(56, 64)}

    def step(c, call, *args):
        call(*args).then_inc(S["v" + c], 1)
        done[c] += 1

    def shifts(c, places, src):
        for i in places:
            step(c, v.tensor_scalar, T.un[0:64, 8 * i:8 * i + 8], src[0:64, :], SH[levels[i]], None, shr)

    def link(c, i):
        z = cols[c]
        v.wait_ge(S["v" + c], done[c])
        if i == 0:
            for j in range(2):
                step(c, v.tensor_tensor, T.mn[0:32, j, z], T.un[quad(j), z], T.ab[quad(j), z], mult)
        elif i == 1:
            step(c, v.tensor_tensor, T.an[0:32, z], T.mn[0:32, 0, z], T.mn[0:32, 1, z], add)
        elif i == 2:
            step(c, v.tensor_scalar, T.bn[0:32, z], T.an[0:32, z], 255, None, band)
        else:
            for t in range(4):
                v.tensor_copy(T.off[quad(t), z], T.bn[0:32, z]).then_inc(S["on" + c], 1)

    v.memset(T.xy[64:128, :], 0).then_inc(S.xf, 1)
    v.memset(T.w0[:, :], 0.0).then_inc(S.z0, 1)
    v.memset(T.e[:, 0:1024], 0.0).then_inc(S.ze0, 1)
    v.wait_ge(S.xy, 64)
    shifts("a", (0, 1), T.xy)
    shifts("b", (2, 3), T.xy)
    v.wait_ge(S.aba, 2)
    link("a", 0)
    shifts("b", (4, 5), T.xy)
    link("a", 1)
    shifts("b", (6,), T.xy)
    v.wait_ge(S.abb, 6)
    link("a", 2)
    link("b", 0)
    link("a", 3)
    for i in (1, 2, 3):
        link("b", i)

    def stat(s, h, m):
        v.wait_ge(S["l%d%d" % (s, h)], m)
        v.quantize_mx(T["s%d%dq" % (s, h)][:, 0:512], T["s%d%ds" % (s, h)][:, 0:512], T["w%d" % h][:, 0:2048]).then_inc(S["q%d%d" % (s, h)], 1)

    def gather(u):
        if u in (0, 4):
            sc.wait_ge(S.onb if u == 0 else S.onc, 4)
            ls = T.off[:, 48:56] if u == 0 else T.off[:, 56:64]
        else:
            sc.wait_ge(S["a%d" % units[u]], len(for_lists[slot(units[u], r)]))
            ls = T.arr[:, 8 * u:8 * u + 8]
        sc.activation(T.ga[:, 128 * u:128 * u + 128], T.wn[:, 0:256].indirect(ls), copy).then_inc(S["g%d" % u], 1)

    def spread(on_vector, u, ts):
        a, queue = 512 * (u % 3), v if on_vector else sc
        if u < 3:
            queue.wait_ge(S.ze2, 1)
        else:
            queue.wait_ge(S["eq%d" % (u - 3)], 1)
        queue.wait_ge(S["g%d" % u], 1)
        for t in ts:
            to, src = T.e[quad(k), a + t:a + 512:4], T.ga[quad(t), 128 * u:128 * u + 128]
            (v.tensor_copy(to, src) if on_vector else sc.activation(to, src, copy)).then_inc(S["c%d" % u], 1)

    def pack(u):
        a = 512 * (u % 3)
        v.wait_ge(S["c%d" % u], 4)
        cq, cs, c = (T.rq, T.rs, r) if u == 0 else (T.eq, T.es, u)
        v.quantize_mx(cq[:, 128 * c:128 * c + 128], cs[:, 128 * c:128 * c + 128], T.e[:, a:a + 512]).then_inc(S["eq%d" % u], 1)

    stat(Q, 0, 32)
    stat(Q, 1, 80)
    v.wait_ge(S.xr, len(every))
    shifts("c", (7,), T.xr)
    spread(True, 0, (0, 1, 2))
    link("c", 0)
    pack(0)
    link("c", 1)
    spread(True, 1, (0, 1, 2, 3))
    link("c", 2)
    pack(1)
    spread(True, 2, (0, 1, 2, 3))
    link("c", 3)
    pack(2)
    spread(True, 3, (0, 1, 2))
    spread(True, 5, (0, 1))
    pack(3)
    spread(True, 5, (2,))
    spread(True, 4, (0, 1, 2, 3))
    pack(5)
    spread(True, 6, (0, 1))
    pack(4)
    spread(True, 6, (2,))
    spread(True, 7, (0, 1))
    pack(6)
    stat(F, 0, 32)
    pack(7)
    stat(F, 1, 48)

    sc.wait_ge(S.ze0, 1)
    sc.activation(T.e[:, 1024:1536], T.e[:, 0:512], copy).then_inc(S.ze2, 1)
    sc.wait_ge(S.st, 32)
    for t in range(4):
        sc.activation(T.wn[quad(t), :], T.st[0:32, t:1024:4], copy).then_inc(S.sp, 1)
    sc.wait_ge(S.sp, 4)
    gather(0)
    spread(False, 0, (3,))
    for u in (1, 2, 3, 5):
        gather(u)
    spread(False, 3, (3,))
    gather(6)
    gather(4)
    spread(False, 5, (3,))
    gather(7)
    spread(False, 6, (3,))
    spread(False, 7, (3, 2))

    def finish(call, o, h, *more):
        i = 2 * o + h
        call(T.yo[:, 128 * i:128 * i + 128], T.ps[:, 512 * i:512 * i + 128], *more).then_inc(S["y%d" % o], 1)

    for o in range(4):
        sc.wait_ge(S["f%d" % (2 * o)], 1)
        finish(sc.activation, o, 0, copy)
        v.wait_ge(S["f%d" % (2 * o + 1)], 1)
        finish(v.tensor_copy, o, 1)

    te = g.tensor
    last = units[7]

    def product(q, o, b):
        i, w, s = 2 * o + (q + b + 1) % 2, slice(128 * o, 128 * o + 128), "s%d%d" % (q // 4, b)
        c = te.matmul_mx(T.ps[:, 512 * i:512 * i + 128], T[s + "q"][:, w], T[s + "s"][:, w],
                         T.rq[:, 128 * q:128 * q + 128], T.rs[:, 128 * q:128 * q + 128], q == r, q == last)
        if q == last:
            c.then_inc(S["f%d" % i], 1)

    def arrived(q):
        te.wait_ge(S["n%d" % q], 2 * len(for_codes[slot(q, r)]))

    def products(q, bs):
        for b in bs:
            for o in range(4):
                product(q, o, b)

    te.wait_ge(S.eq0, 1)
    for b in range(2):
        te.wait_ge(S["q%d%d" % (Q, b)], 1)
        products(r, [b])
    for q in units[1:3] + [partner]:
        arrived(q)
        products(q, [0, 1])
    te.wait_ge(S["q%d0" % F], 1)
    for q in (units[3], units[5]):
        arrived(q)
        products(q, [0])
    te.wait_ge(S["q%d1" % F], 1)
    for q in (units[3], units[5]):
        products(q, [1])
    arrived(units[6])
    products(units[6], [0, 1])
    arrived(last)
    for o in range(4):
        for h in range(2):
            product(last, o, (last + h + 1) % 2)

    for o in range(4):
        g.sync.wait_ge(S["y%d" % o], 2)
        g.sync.dma_start(T.y[:, 256 * o:256 * o + 256], T.yo[:, 256 * o:256 * o + 256]).then_inc(S.yd, 16)
    g.sync.wait_ge(S.yd, 64)
